import numpy as np
import ml_dtypes


def mxq(x, axis, fmt="e4m3"):
    dtype, down = {"e4m3": (ml_dtypes.float8_e4m3fn, 7), "e5m2": (ml_dtypes.float8_e5m2, 14)}[fmt]
    v = np.moveaxis(np.asarray(x, np.float32).astype(ml_dtypes.bfloat16).astype(np.float64), axis, -1)
    blocks = v.reshape(v.shape[:-1] + (-1, 32))
    amax = np.abs(blocks).max(-1, keepdims=True)
    byte = np.maximum(np.where(amax > 0, np.frexp(amax)[1] - 1 + 127, 0) - down, 1)
    scale = np.exp2(byte - 127.0)
    codes = (blocks / scale).astype(np.float32).astype(dtype).astype(np.float64)
    return np.moveaxis((codes * scale).reshape(v.shape), -1, axis)


WIDE = False


def mx_kscale(k):
    if not WIDE:
        return np.ones(k)
    levels = np.array([10, -10, 5, -5, 0])
    if k % 512:
        return np.exp2(np.random.permutation(np.resize(levels, k // 32))).repeat(32)
    a = np.empty((k // 512, 16))
    for p in range(k // 512):
        a[p, :8] = np.random.permutation(np.resize(levels, 8))
        for g in range(8):
            far = levels[np.abs(levels - a[p, g]) >= 10]
            a[p, g + 8] = far[np.random.randint(len(far))]
    return np.exp2(a.ravel()).repeat(32)


def f64(x):
    return np.asarray(x).astype(np.float64)


def striped(idx):
    return np.tile(idx.reshape(-1, 16).T, (8, 1)).astype(np.uint16)


def unstriped(offs):
    return offs[:16].T.reshape(-1).astype(np.int64)


def striped8(idx):
    return np.concatenate([x.reshape(-1, 16).T for x in idx]).astype(np.uint16)


def runs(offs, k):
    lists = np.stack([offs[16 * r : 16 * r + 16].T.reshape(-1) for r in range(8)]).astype(np.int64)
    return lists[np.arange(k) % 512 // 64]


def pack_weight(w):
    k, n = w.shape
    w = f64(np.asarray(w, np.float32).astype(ml_dtypes.bfloat16)).reshape(k // 32, 32, n)
    amax = np.abs(w).max(1)
    byte = np.clip(np.where(amax > 0, np.frexp(amax)[1] - 1 + 127 - 7, 1), 1, 254)
    scaled = (w * np.exp2(127.0 - byte)[:, None, :]).reshape(k, n).astype(np.float32)
    words = np.ascontiguousarray(scaled.reshape(k // 512, 128, 4, n).transpose(0, 1, 3, 2)).astype(ml_dtypes.float8_e4m3fn).view(np.uint8)
    return words, np.ascontiguousarray(byte.astype(np.uint8).reshape(k // 512, 16, n))


def unpack_weight(words, scales):
    g, p, n, _ = words.shape
    vals = np.ascontiguousarray(words).view(ml_dtypes.float8_e4m3fn).astype(np.float64) * np.repeat(np.exp2(scales.astype(np.float64) - 127.0), 8, axis=1)[..., None]
    return vals.transpose(0, 1, 3, 2).reshape(g * 512, n)


def sigmoid(v):
    return 1.0 / (1.0 + np.exp(-np.maximum(v, -700.0)))

def planes(y):
    n, m = y.shape
    v = y.astype(np.float32).astype(ml_dtypes.bfloat16).astype(np.float64).reshape(n // 32, 32, m)
    top = np.abs(v).max(1)
    byte = np.clip(np.where(top > 0, np.frexp(top)[1] - 1 + 127 - 7, 1), 1, 254)
    codes = (v * np.exp2(127.0 - byte)[:, None, :]).reshape(n, m).astype(np.float32).astype(ml_dtypes.float8_e4m3fn).view(np.uint8)
    words = codes.reshape(n // 512, 128, 4, m).transpose(0, 1, 3, 2)
    return np.ascontiguousarray(words), np.ascontiguousarray(byte.astype(np.uint8).reshape(n // 512, 16, m))


K, T, S, N, H, J = 512, 2048, 512, 512, 512, 512


def setup_inputs():
    n = np.random.standard_normal
    s = mx_kscale(K)[:, None]
    u = mx_kscale(H)
    packed_xT = pack_weight(n((K, T)) * s)
    packed_w1 = pack_weight(n((K, H)) / np.sqrt(K) / s)
    packed_w2 = pack_weight(n((K, H)) / np.sqrt(K) / s)
    packed_w3 = pack_weight(n((H, N)) / np.sqrt(H) / u[:, None])
    return {
        "x_words": packed_xT[0],
        "x_scales": packed_xT[1],
        "w1_words": packed_w1[0],
        "w1_scales": packed_w1[1],
        "w2_words": packed_w2[0],
        "w2_scales": packed_w2[1],
        "gn": (np.random.uniform(0.5, 1.5, (H, 1)) * u[:, None]).astype(np.float32),
        "w3_words": packed_w3[0],
        "w3_scales": packed_w3[1],
        "tab": n((N, J)).astype(np.float32),
        "offs": striped(np.random.permutation(T)[:S]),
        "hz": striped8(np.random.randint(0, T, (8, S))),
        "n1": striped8(np.stack([np.random.permutation(S) for _ in range(8)])),
        "n2": striped8(np.stack([np.random.permutation(S) for _ in range(8)])),
        "n3": striped(np.random.randint(0, J, S)),
        "n4": striped(np.random.permutation(S)),
    }


def reference(x_words, x_scales, w1_words, w1_scales, w2_words, w2_scales, gn, w3_words, w3_scales, tab, offs, hz, n1, n2, n3, n4):
    xq = unpack_weight(x_words, x_scales)[:, unstriped(offs)]
    y = unpack_weight(w1_words, w1_scales).T @ xq
    x_hz = unpack_weight(x_words, x_scales)[np.arange(K)[:, None], runs(hz, K)]
    d = unpack_weight(w2_words, w2_scales).T @ x_hz
    z = f64(gn) * (y + (sigmoid(d[np.arange(H)[:, None], runs(n2, H)] - d)) * (y[np.arange(H)[:, None], runs(n1, H)] - y))
    h = unpack_weight(w3_words, w3_scales).T @ mxq(z, 0, "e4m3")
    out_0 = np.maximum(h + f64(tab)[:, unstriped(n3)], h[:, unstriped(n4)])
    return (out_0,) + planes(out_0)

@@ -1,0 +1,249 @@
+from contextlib import ExitStack
+
+import concourse.mybir as mybir
+
+F32 = mybir.dt.float32
+BF16 = mybir.dt.bfloat16
+I32 = mybir.dt.int32
+U32 = mybir.dt.uint32
+U16 = mybir.dt.uint16
+U8 = mybir.dt.uint8
+FP8X4 = mybir.dt.float8_e4m3fn_x4
+ALU = mybir.AluOpType
+ACT = mybir.ActivationFunctionType
+
+P = 128
+T = 2048
+S = 512
+HALF = S // 2
+EARLY_Y = 2
+FLOPS = 3 * 2 * 512 * 512 * 512
+
+
+def tile_picked_twhpullbkind_none_po_kernel(
+    tc, x_words, x_scales, w1_words, w1_scales, w2_words, w2_scales, gn, w3_words, w3_scales, tab,
+    offs, hz, n1, n2, n3, n4, out_0, out_1, out_2,
+):
+    nc = tc.nc
+    with ExitStack() as ctx:
+        lists = ctx.enter_context(tc.tile_pool(name="lists", bufs=1))
+        keep = ctx.enter_context(tc.tile_pool(name="keep", bufs=1))
+        shared = ctx.enter_context(tc.tile_pool(name="shared", bufs=1))
+        psum = ctx.enter_context(tc.psum_pool(name="psum", bufs=1))
+
+        def words_view(dram):
+            return dram[0].rearrange("p c r -> p (c r)").bitcast(I32)
+
+        def load_list(dram, name):
+            tile = lists.tile([P, S // 16], U16, name=name)
+            nc.sync.dma_start(tile[:], dram)
+            return tile
+
+        def half_cols(hf):
+            return slice(hf * HALF, (hf + 1) * HALF)
+
+        def half_list(tile, hf):
+            return tile[:, hf * HALF // 16 : (hf + 1) * HALF // 16]
+
+        xs = shared.tile([P, T], U8, name="xs", offset=4 * T + T // 2)
+        ws_raw = keep.tile([P, 3, S], U8, name="ws_raw")
+        hz_scale = keep.tile([P, S], U8, name="hz_scale", align_bytes=64)
+        nc.gpsimd.memset(xs[:].bitcast(I32), 0)
+        nc.vector.memset(ws_raw[:].bitcast(I32), 0)
+        nc.vector.memset(hz_scale[:].bitcast(I32), 0)
+
+        def load_scale_rows(engine, which, dram):
+            rows = dram[0].bitcast(I32)
+            for q in range(4):
+                engine.dma_start(ws_raw[32 * q : 32 * q + 4, which, :].bitcast(I32), rows[4 * q : 4 * q + 4, :])
+
+        xw = shared.tile([P, T], I32, name="xw", offset=0)
+        nc.gpsimd.dma_start(xw[:], words_view(x_words))
+
+        hz_t = load_list(hz, "hz_t")
+        xs_rows = x_scales[0].bitcast(I32)
+        for r in range(4):
+            nc.sync.dma_start(
+                xs[r:P:16, :].bitcast(I32), xs_rows[r:16:4, :].unsqueeze(1).to_broadcast([4, 2, T // 4])
+            )
+        offs_t = load_list(offs, "offs_t")
+        load_scale_rows(nc.sync, 0, w1_scales)
+        w1_raw = shared.tile([P, S], I32, name="w1_raw", offset=6 * T)
+        nc.sync.dma_start(w1_raw[:], words_view(w1_words))
+        w2_raw = shared.tile([P, S], I32, name="w2_raw", offset=7 * T)
+        nc.sync.dma_start(w2_raw[:], words_view(w2_words))
+        gain = keep.tile([P, 4], F32, name="gain")
+        nc.sync.dma_start(gain[:], gn.rearrange("(p t) o -> p (t o)", t=4))
+        load_scale_rows(nc.sync, 1, w2_scales)
+
+        hz_bytes = keep.tile([P, S], U8, name="hz_bytes")
+        nc.vector.tensor_copy(hz_bytes[:], xs[:].indirect(hz_t[:]))
+        for r in range(4):
+            src = r if r < 2 else 16 + r
+            nc.sync.dma_start(hz_scale[r:P:32, :].bitcast(I32), hz_bytes[src:P:32, :].bitcast(I32))
+        n2_t = load_list(n2, "n2_t")
+        n1_t = load_list(n1, "n1_t")
+        n3_t = load_list(n3, "n3_t")
+        n4_t = load_list(n4, "n4_t")
+        idx_scale = keep.tile([P, S], U8, name="idx_scale", align_bytes=64)
+        nc.vector.tensor_copy(idx_scale[:], xs[:].indirect(offs_t[:]))
+        idx_codes = shared.tile([P, S], U32, name="idx_codes", align_bytes=64, offset=4 * T)
+        nc.vector.tensor_copy(idx_codes[:], xw[:].bitcast(U32).indirect(offs_t[:]))
+        hz_codes = shared.tile([P, S], U32, name="hz_codes", align_bytes=64, offset=5 * T)
+        nc.vector.tensor_copy(hz_codes[:], xw[:].bitcast(U32).indirect(hz_t[:]))
+
+        def dealt(ap, run):
+            return ap.rearrange("p (t c i) -> p c t i", t=4, i=run)
+
+        def undealt(ap, run):
+            return ap.rearrange("p (c i t) -> p c t i", t=4, i=run)
+
+        def deal_words(raw, name):
+            codes = keep.tile([P, S], U32, name=name, align_bytes=64)
+            nc.scalar.copy(dealt(codes[:], 4), undealt(raw[:].bitcast(U32), 4))
+            return codes
+
+        def deal_bytes(which, name):
+            plane = keep.tile([P, S], U8, name=name, align_bytes=64)
+            nc.gpsimd.tensor_copy(dealt(plane[:], 16), undealt(ws_raw[:, which, :], 16))
+            return plane
+
+        w1_codes = deal_words(w1_raw, "w1_codes")
+        ws1 = deal_bytes(0, "ws1")
+        w2_codes = deal_words(w2_raw, "w2_codes")
+        ws2 = deal_bytes(1, "ws2")
+
+        w3_raw = shared.tile([P, S], I32, name="w3_raw", offset=6 * T)
+        nc.sync.dma_start(w3_raw[:], words_view(w3_words))
+        load_scale_rows(nc.sync, 2, w3_scales)
+        tab_rows = tab.rearrange("(p t) j -> p t j", t=4)
+        tab_win = []
+        for t in range(4):
+            tile = shared.tile([P, S], F32, name=f"tab{t}", offset=4 * S * t)
+            nc.sync.dma_start(tile[:], tab_rows[:, t, :])
+            tab_win.append(tile)
+
+        def product(target, w_codes, w_plane, t, codes, plane):
+            m = slice(P * t, P * (t + 1))
+            nc.tensor.matmul_mx(
+                target, lhsT=w_codes[:, m].bitcast(FP8X4), lhsT_scale=w_plane[:, m],
+                rhs=codes[:].bitcast(FP8X4), rhs_scale=plane[:], start=True, stop=True,
+            )
+
+        d_bank = [psum.tile([P, S], F32, name=f"d_bank{t}", tag=f"dh{t}") for t in range(4)]
+        y_bank = [psum.tile([P, S], F32, name=f"y_bank{t}", tag=f"yh{t}") for t in range(4)]
+        for t in range(EARLY_Y):
+            product(y_bank[t][:], w1_codes, ws1, t, idx_codes, idx_scale)
+        for t in range(4):
+            if t >= EARLY_Y:
+                product(y_bank[t][:], w1_codes, ws1, t, idx_codes, idx_scale)
+            product(d_bank[t][:], w2_codes, ws2, t, hz_codes, hz_scale)
+
+        w3_codes = keep.tile([P, S], U32, name="w3_codes", align_bytes=64)
+        nc.gpsimd.tensor_copy(dealt(w3_codes[:], 4), undealt(w3_raw[:].bitcast(U32), 4))
+        ws3 = deal_bytes(2, "ws3")
+
+        d_win = [keep.tile([P, S], F32, name=f"d_win{t}") for t in range(4)]
+        y_win = [shared.tile([P, S], F32, name=f"y_win{t}", offset=7 * T + 4 * S * t) for t in range(4)]
+        d_far = keep.tile([P, 4, S], F32, name="d_far")
+        d_diff = keep.tile([P, 4, S], F32, name="d_diff", tag="diff_tab")
+        gate = keep.tile([P, 4, S], F32, name="gate")
+        far_part = keep.tile([P, 4, S], F32, name="far_part")
+        own_part = keep.tile([P, 4, S], F32, name="own_part")
+
+        def leave_bank_y(t):
+            nc.scalar.activation(y_win[t][:], y_bank[t][:], ACT.Copy, scale=gain[:, t : t + 1])
+
+        for t in range(EARLY_Y):
+            leave_bank_y(t)
+
+        def first_steps(t):
+            if t == 0:
+                nc.vector.tensor_copy(d_win[t][:], d_bank[t][:])
+            else:
+                nc.scalar.copy(d_win[t][:], d_bank[t][:])
+            for hf in range(2):
+                window = d_win[t][:].indirect(half_list(n2_t, hf))
+                if t == 0:
+                    nc.vector.tensor_copy(d_far[:, t, half_cols(hf)], window)
+                else:
+                    nc.scalar.activation(d_far[:, t, half_cols(hf)], window, ACT.Copy)
+            nc.vector.tensor_tensor(d_diff[:, t, :], d_far[:, t, :], d_bank[t][:], ALU.subtract)
+
+        def second_steps(t):
+            if t >= EARLY_Y:
+                leave_bank_y(t)
+            nc.scalar.activation(gate[:, t, :], d_diff[:, t, :], ACT.Sigmoid)
+            for hf in range(2):
+                cols = half_cols(hf)
+                nc.vector.tensor_tensor(
+                    far_part[:, t, cols], y_win[t][:].indirect(half_list(n1_t, hf)), gate[:, t, cols], ALU.mult
+                )
+            nc.vector.scalar_tensor_tensor(
+                own_part[:, t, :], gate[:, t, :], 1.0, y_win[t][:], ALU.subtract, ALU.mult
+            )
+
+        for t in range(5):
+            if t < 4:
+                first_steps(t)
+            if t > 0:
+                second_steps(t - 1)
+
+        tab_far = keep.tile([P, 4, S], F32, name="tab_far", tag="diff_tab")
+        for hf in range(2):
+            for t in range(4):
+                nc.scalar.activation(tab_far[:, t, half_cols(hf)], tab_win[t][:].indirect(half_list(n3_t, hf)), ACT.Copy)
+
+        def woven(tile):
+            return tile[:].rearrange("p (c i) t -> p c t i", i=4)
+
+        def planes_of(tile, cols):
+            return tile[:, :, cols].rearrange("p t (c i) -> p c t i", i=4)
+
+        def quantise(codes, plane, grouped):
+            nc.vector.quantize_mx(codes.bitcast(FP8X4), plane, grouped[:].rearrange("p j t -> p (j t)"))
+
+        z_bf = [keep.tile([P, HALF, 4], BF16, name=f"z_bf{hf}", align_bytes=64) for hf in range(2)]
+        z_codes = [keep.tile([P, HALF], U32, name=f"z_codes{hf}", align_bytes=64) for hf in range(2)]
+        z_plane = [keep.tile([P, HALF], U8, name=f"z_plane{hf}", align_bytes=64) for hf in range(2)]
+        h_bank = [
+            [psum.tile([P, HALF], F32, name=f"h_bank{hf}{t}", tag=f"{('yh', 'dh')[hf]}{t}") for t in range(4)]
+            for hf in range(2)
+        ]
+        for hf in range(2):
+            cols = half_cols(hf)
+            nc.vector.tensor_tensor(woven(z_bf[hf]), planes_of(far_part, cols), planes_of(own_part, cols), ALU.subtract)
+            quantise(z_codes[hf][:], z_plane[hf][:], z_bf[hf])
+            for t in range(4):
+                product(h_bank[hf][t][:], w3_codes, ws3, t, z_codes[hf], z_plane[hf])
+
+        h_win = [keep.tile([P, S], F32, name=f"h_win{t}") for t in range(4)]
+        h_far = keep.tile([P, 4, S], F32, name="h_far")
+        h_sum = keep.tile([P, 4, S], F32, name="h_sum")
+        result = [keep.tile([P, 4, HALF], F32, name=f"result{hf}") for hf in range(2)]
+        out_bf = [keep.tile([P, HALF, 4], BF16, name=f"out_bf{hf}", align_bytes=64) for hf in range(2)]
+        out_codes = [keep.tile([P, HALF], U32, name=f"out_codes{hf}", align_bytes=64) for hf in range(2)]
+        out_plane = keep.tile([P, S], U8, name="out_plane", align_bytes=64)
+        for hf in range(2):
+            cols = half_cols(hf)
+            for t in range(4):
+                nc.vector.tensor_tensor(h_sum[:, t, cols], tab_far[:, t, cols], h_bank[hf][t][:], ALU.add)
+                nc.scalar.copy(h_win[t][:, cols], h_bank[hf][t][:])
+        out_rows = out_0.rearrange("(p t) j -> p t j", t=4)
+        for hf in range(2):
+            cols = half_cols(hf)
+            for t in range(4):
+                window = h_win[t][:].indirect(half_list(n4_t, hf))
+                if t == 0 and hf == 1:
+                    nc.vector.tensor_copy(h_far[:, t, cols], window)
+                else:
+                    nc.scalar.activation(h_far[:, t, cols], window, ACT.Copy)
+                nc.vector.tensor_tensor(result[hf][:, t, :], h_sum[:, t, cols], h_far[:, t, cols], ALU.max)
+            nc.sync.dma_start(out_rows[:, :, cols], result[hf][:])
+            nc.vector.tensor_copy(woven(out_bf[hf]), planes_of(result[hf], slice(0, HALF)))
+            quantise(out_codes[hf][:], out_plane[:, cols], out_bf[hf])
+            nc.sync.dma_start(words_view(out_1)[:, cols], out_codes[hf][:].bitcast(I32))
+        out_scale_rows = out_2[0].bitcast(I32)
+        for q in range(4):
+            engine = nc.scalar if q % 2 else nc.sync
+            engine.dma_start(out_scale_rows[4 * q : 4 * q + 4, :], out_plane[32 * q : 32 * q + 4, :].bitcast(I32))

@@ -45,6 +45,10 @@ def tile_picked_twhpullbkind_none_po_kernel(
         def half_list(tile, hf):
             return tile[:, hf * HALF // 16 : (hf + 1) * HALF // 16]
 
+        warm = keep.tile([P, 2], F32, name="warm")
+        nc.gpsimd.memset(warm[:, 0:1], 0.0)
+        nc.scalar.activation(warm[:, 1:2], warm[:, 0:1], ACT.Sigmoid)
+
         xs = shared.tile([P, T], U8, name="xs", offset=4 * T + T // 2)
         ws_raw = keep.tile([P, 3, S], U8, name="ws_raw")
         hz_scale = keep.tile([P, S], U8, name="hz_scale", align_bytes=64)

from contextlib import ExitStack

import concourse.mybir as mybir

F32 = mybir.dt.float32
BF16 = mybir.dt.bfloat16
I32 = mybir.dt.int32
U32 = mybir.dt.uint32
U16 = mybir.dt.uint16
U8 = mybir.dt.uint8
FP8X4 = mybir.dt.float8_e4m3fn_x4
ALU = mybir.AluOpType
ACT = mybir.ActivationFunctionType

P = 128
T = 2048
S = 512
HALF = S // 2
EARLY_Y = 2
FLOPS = 3 * 2 * 512 * 512 * 512


def tile_picked_twhpullbkind_none_po_kernel(
    tc, x_words, x_scales, w1_words, w1_scales, w2_words, w2_scales, gn, w3_words, w3_scales, tab,
    offs, hz, n1, n2, n3, n4, out_0, out_1, out_2,
):
    nc = tc.nc
    with ExitStack() as ctx:
        lists = ctx.enter_context(tc.tile_pool(name="lists", bufs=1))
        keep = ctx.enter_context(tc.tile_pool(name="keep", bufs=1))
        shared = ctx.enter_context(tc.tile_pool(name="shared", bufs=1))
        psum = ctx.enter_context(tc.psum_pool(name="psum", bufs=1))

        def words_view(dram):
            return dram[0].rearrange("p c r -> p (c r)").bitcast(I32)

        def load_list(dram, name):
            tile = lists.tile([P, S // 16], U16, name=name)
            nc.sync.dma_start(tile[:], dram)
            return tile

        def half_cols(hf):
            return slice(hf * HALF, (hf + 1) * HALF)

        def half_list(tile, hf):
            return tile[:, hf * HALF // 16 : (hf + 1) * HALF // 16]

        warm = keep.tile([P, 2], F32, name="warm")
        nc.gpsimd.memset(warm[:, 0:1], 0.0)
        nc.scalar.activation(warm[:, 1:2], warm[:, 0:1], ACT.Sigmoid)

        xs = shared.tile([P, T], U8, name="xs", offset=4 * T + T // 2)
        ws_raw = keep.tile([P, 3, S], U8, name="ws_raw")
        hz_scale = keep.tile([P, S], U8, name="hz_scale", align_bytes=64)
        nc.gpsimd.memset(xs[:].bitcast(I32), 0)
        nc.vector.memset(ws_raw[:].bitcast(I32), 0)
        nc.vector.memset(hz_scale[:].bitcast(I32), 0)

        def load_scale_rows(engine, which, dram):
            rows = dram[0].bitcast(I32)
            for q in range(4):
                engine.dma_start(ws_raw[32 * q : 32 * q + 4, which, :].bitcast(I32), rows[4 * q : 4 * q + 4, :])

        xw = shared.tile([P, T], I32, name="xw", offset=0)
        nc.gpsimd.dma_start(xw[:], words_view(x_words))

        hz_t = load_list(hz, "hz_t")
        xs_rows = x_scales[0].bitcast(I32)
        for r in range(4):
            nc.sync.dma_start(
                xs[r:P:16, :].bitcast(I32), xs_rows[r:16:4, :].unsqueeze(1).to_broadcast([4, 2, T // 4])
            )
        offs_t = load_list(offs, "offs_t")
        load_scale_rows(nc.sync, 0, w1_scales)
        w1_raw = shared.tile([P, S], I32, name="w1_raw", offset=6 * T)
        nc.sync.dma_start(w1_raw[:], words_view(w1_words))
        w2_raw = shared.tile([P, S], I32, name="w2_raw", offset=7 * T)
        nc.sync.dma_start(w2_raw[:], words_view(w2_words))
        gain = keep.tile([P, 4], F32, name="gain")
        nc.sync.dma_start(gain[:], gn.rearrange("(p t) o -> p (t o)", t=4))
        load_scale_rows(nc.sync, 1, w2_scales)

        hz_bytes = keep.tile([P, S], U8, name="hz_bytes")
        nc.vector.tensor_copy(hz_bytes[:], xs[:].indirect(hz_t[:]))
        for r in range(4):
            src = r if r < 2 else 16 + r
            nc.sync.dma_start(hz_scale[r:P:32, :].bitcast(I32), hz_bytes[src:P:32, :].bitcast(I32))
        n2_t = load_list(n2, "n2_t")
        n1_t = load_list(n1, "n1_t")
        n3_t = load_list(n3, "n3_t")
        n4_t = load_list(n4, "n4_t")
        idx_scale = keep.tile([P, S], U8, name="idx_scale", align_bytes=64)
        nc.vector.tensor_copy(idx_scale[:], xs[:].indirect(offs_t[:]))
        idx_codes = shared.tile([P, S], U32, name="idx_codes", align_bytes=64, offset=4 * T)
        nc.vector.tensor_copy(idx_codes[:], xw[:].bitcast(U32).indirect(offs_t[:]))
        hz_codes = shared.tile([P, S], U32, name="hz_codes", align_bytes=64, offset=5 * T)
        nc.vector.tensor_copy(hz_codes[:], xw[:].bitcast(U32).indirect(hz_t[:]))

        def dealt(ap, run):
            return ap.rearrange("p (t c i) -> p c t i", t=4, i=run)

        def undealt(ap, run):
            return ap.rearrange("p (c i t) -> p c t i", t=4, i=run)

        def deal_words(raw, name):
            codes = keep.tile([P, S], U32, name=name, align_bytes=64)
            nc.scalar.copy(dealt(codes[:], 4), undealt(raw[:].bitcast(U32), 4))
            return codes

        def deal_bytes(which, name):
            plane = keep.tile([P, S], U8, name=name, align_bytes=64)
            nc.gpsimd.tensor_copy(dealt(plane[:], 16), undealt(ws_raw[:, which, :], 16))
            return plane

        w1_codes = deal_words(w1_raw, "w1_codes")
        ws1 = deal_bytes(0, "ws1")
        w2_codes = deal_words(w2_raw, "w2_codes")
        ws2 = deal_bytes(1, "ws2")

        w3_raw = shared.tile([P, S], I32, name="w3_raw", offset=6 * T)
        nc.sync.dma_start(w3_raw[:], words_view(w3_words))
        load_scale_rows(nc.sync, 2, w3_scales)
        tab_rows = tab.rearrange("(p t) j -> p t j", t=4)
        tab_win = []
        for t in range(4):
            tile = shared.tile([P, S], F32, name=f"tab{t}", offset=4 * S * t)
            nc.sync.dma_start(tile[:], tab_rows[:, t, :])
            tab_win.append(tile)

        def product(target, w_codes, w_plane, t, codes, plane):
            m = slice(P * t, P * (t + 1))
            nc.tensor.matmul_mx(
                target, lhsT=w_codes[:, m].bitcast(FP8X4), lhsT_scale=w_plane[:, m],
                rhs=codes[:].bitcast(FP8X4), rhs_scale=plane[:], start=True, stop=True,
            )

        d_bank = [psum.tile([P, S], F32, name=f"d_bank{t}", tag=f"dh{t}") for t in range(4)]
        y_bank = [psum.tile([P, S], F32, name=f"y_bank{t}", tag=f"yh{t}") for t in range(4)]
        for t in range(EARLY_Y):
            product(y_bank[t][:], w1_codes, ws1, t, idx_codes, idx_scale)
        for t in range(4):
            if t >= EARLY_Y:
                product(y_bank[t][:], w1_codes, ws1, t, idx_codes, idx_scale)
            product(d_bank[t][:], w2_codes, ws2, t, hz_codes, hz_scale)

        w3_codes = keep.tile([P, S], U32, name="w3_codes", align_bytes=64)
        nc.gpsimd.tensor_copy(dealt(w3_codes[:], 4), undealt(w3_raw[:].bitcast(U32), 4))
        ws3 = deal_bytes(2, "ws3")

        d_win = [keep.tile([P, S], F32, name=f"d_win{t}") for t in range(4)]
        y_win = [shared.tile([P, S], F32, name=f"y_win{t}", offset=7 * T + 4 * S * t) for t in range(4)]
        d_far = keep.tile([P, 4, S], F32, name="d_far")
        d_diff = keep.tile([P, 4, S], F32, name="d_diff", tag="diff_tab")
        gate = keep.tile([P, 4, S], F32, name="gate")
        far_part = keep.tile([P, 4, S], F32, name="far_part")
        own_part = keep.tile([P, 4, S], F32, name="own_part")

        def leave_bank_y(t):
            nc.scalar.activation(y_win[t][:], y_bank[t][:], ACT.Copy, scale=gain[:, t : t + 1])

        for t in range(EARLY_Y):
            leave_bank_y(t)

        def first_steps(t):
            if t == 0:
                nc.vector.tensor_copy(d_win[t][:], d_bank[t][:])
            else:
                nc.scalar.copy(d_win[t][:], d_bank[t][:])
            for hf in range(2):
                window = d_win[t][:].indirect(half_list(n2_t, hf))
                if t == 0:
                    nc.vector.tensor_copy(d_far[:, t, half_cols(hf)], window)
                else:
                    nc.scalar.activation(d_far[:, t, half_cols(hf)], window, ACT.Copy)
            nc.vector.tensor_tensor(d_diff[:, t, :], d_far[:, t, :], d_bank[t][:], ALU.subtract)

        def second_steps(t):
            if t >= EARLY_Y:
                leave_bank_y(t)
            nc.scalar.activation(gate[:, t, :], d_diff[:, t, :], ACT.Sigmoid)
            for hf in range(2):
                cols = half_cols(hf)
                nc.vector.tensor_tensor(
                    far_part[:, t, cols], y_win[t][:].indirect(half_list(n1_t, hf)), gate[:, t, cols], ALU.mult
                )
            nc.vector.scalar_tensor_tensor(
                own_part[:, t, :], gate[:, t, :], 1.0, y_win[t][:], ALU.subtract, ALU.mult
            )

        for t in range(5):
            if t < 4:
                first_steps(t)
            if t > 0:
                second_steps(t - 1)

        tab_far = keep.tile([P, 4, S], F32, name="tab_far", tag="diff_tab")
        for hf in range(2):
            for t in range(4):
                nc.scalar.activation(tab_far[:, t, half_cols(hf)], tab_win[t][:].indirect(half_list(n3_t, hf)), ACT.Copy)

        def woven(tile):
            return tile[:].rearrange("p (c i) t -> p c t i", i=4)

        def planes_of(tile, cols):
            return tile[:, :, cols].rearrange("p t (c i) -> p c t i", i=4)

        def quantise(codes, plane, grouped):
            nc.vector.quantize_mx(codes.bitcast(FP8X4), plane, grouped[:].rearrange("p j t -> p (j t)"))

        z_bf = [keep.tile([P, HALF, 4], BF16, name=f"z_bf{hf}", align_bytes=64) for hf in range(2)]
        z_codes = [keep.tile([P, HALF], U32, name=f"z_codes{hf}", align_bytes=64) for hf in range(2)]
        z_plane = [keep.tile([P, HALF], U8, name=f"z_plane{hf}", align_bytes=64) for hf in range(2)]
        h_bank = [
            [psum.tile([P, HALF], F32, name=f"h_bank{hf}{t}", tag=f"{('yh', 'dh')[hf]}{t}") for t in range(4)]
            for hf in range(2)
        ]
        for hf in range(2):
            cols = half_cols(hf)
            nc.vector.tensor_tensor(woven(z_bf[hf]), planes_of(far_part, cols), planes_of(own_part, cols), ALU.subtract)
            quantise(z_codes[hf][:], z_plane[hf][:], z_bf[hf])
            for t in range(4):
                product(h_bank[hf][t][:], w3_codes, ws3, t, z_codes[hf], z_plane[hf])

        h_win = [keep.tile([P, S], F32, name=f"h_win{t}") for t in range(4)]
        h_far = keep.tile([P, 4, S], F32, name="h_far")
        h_sum = keep.tile([P, 4, S], F32, name="h_sum")
        result = [keep.tile([P, 4, HALF], F32, name=f"result{hf}") for hf in range(2)]
        out_bf = [keep.tile([P, HALF, 4], BF16, name=f"out_bf{hf}", align_bytes=64) for hf in range(2)]
        out_codes = [keep.tile([P, HALF], U32, name=f"out_codes{hf}", align_bytes=64) for hf in range(2)]
        out_plane = keep.tile([P, S], U8, name="out_plane", align_bytes=64)
        for hf in range(2):
            cols = half_cols(hf)
            for t in range(4):
                nc.vector.tensor_tensor(h_sum[:, t, cols], tab_far[:, t, cols], h_bank[hf][t][:], ALU.add)
                nc.scalar.copy(h_win[t][:, cols], h_bank[hf][t][:])
        out_rows = out_0.rearrange("(p t) j -> p t j", t=4)
        for hf in range(2):
            cols = half_cols(hf)
            for t in range(4):
                window = h_win[t][:].indirect(half_list(n4_t, hf))
                if t == 0 and hf == 1:
                    nc.vector.tensor_copy(h_far[:, t, cols], window)
                else:
                    nc.scalar.activation(h_far[:, t, cols], window, ACT.Copy)
                nc.vector.tensor_tensor(result[hf][:, t, :], h_sum[:, t, cols], h_far[:, t, cols], ALU.max)
            nc.sync.dma_start(out_rows[:, :, cols], result[hf][:])
            nc.vector.tensor_copy(woven(out_bf[hf]), planes_of(result[hf], slice(0, HALF)))
            quantise(out_codes[hf][:], out_plane[:, cols], out_bf[hf])
            nc.sync.dma_start(words_view(out_1)[:, cols], out_codes[hf][:].bitcast(I32))
        out_scale_rows = out_2[0].bitcast(I32)
        for q in range(4):
            engine = nc.scalar if q % 2 else nc.sync
            engine.dma_start(out_scale_rows[4 * q : 4 * q + 4, :], out_plane[32 * q : 32 * q + 4, :].bitcast(I32))
